import numpy as np
import ml_dtypes

BF16 = ml_dtypes.bfloat16


def bf(x):
    return np.asarray(x, np.float32).astype(BF16)


def f32(x):
    return np.asarray(x, np.float32)


def f64(x):
    return np.asarray(x).astype(np.float64)


def striped(idx):
    return np.tile(idx.reshape(-1, 16).T, (8, 1))


S, K, H, M, N, D, V = 2048, 128, 128, 128, 1536, 4, 384


def setup_inputs():
    return {"x": bf(np.random.standard_normal((K, S))), "w": bf(np.random.standard_normal((K, H)) / np.sqrt(K)), "b": f32(0.5 * np.random.standard_normal((H, 1))), "w2": bf(np.random.standard_normal((H, M)) / np.sqrt(H)), "offs": striped(np.random.permutation(np.tile(np.arange(S), 2))[:N])}


def reference(x, w, b, w2, offs):
    idx = offs[:16].T.reshape(-1)
    t = np.tanh(f64(w).T @ f64(x) + f64(b))
    return (f64(w2).T @ t[:, idx]).reshape(M, V, D).max(axis=2)

@@ -1,0 +1,52 @@
+import concourse.mybir as mybir
+
+BF16, F32, U16 = mybir.dt.bfloat16, mybir.dt.float32, mybir.dt.uint16
+TANH = mybir.ActivationFunctionType.Tanh
+
+P = 128
+S = 2048
+N = 1536
+D = 4
+BANK = 512
+FLOPS = 2 * P * P * (S + N)
+
+
+def tile_rows_gcn2_tanh_max_kernel(tc, x, w, b, w2, offs, out):
+    nc = tc.nc
+    with (
+        tc.tile_pool(name="held", bufs=1) as held,
+        tc.psum_pool(name="psum", bufs=1) as psum,
+    ):
+        w_sb = held.tile([P, P], BF16)
+        b_sb = held.tile([P, 1], F32)
+        w2_sb = held.tile([P, P], BF16)
+        offsets = held.tile([P, N // 16], U16)
+        x_sb = [held.tile([P, BANK], BF16, name=f"x{c}") for c in range(S // BANK)]
+        h = held.tile([P, S], BF16)
+
+        nc.sync.dma_start(w_sb[:], w)
+        nc.scalar.dma_start(b_sb[:], b)
+        for c in range(S // BANK):
+            nc.sync.dma_start(x_sb[c][:], x[:, c * BANK : (c + 1) * BANK])
+        nc.sync.dma_start(w2_sb[:], w2)
+        nc.sync.dma_start(offsets[:], offs)
+
+        warm_in = held.tile([P, 1], F32)
+        warm_out = held.tile([P, 1], F32)
+        nc.vector.memset(warm_in[:], 0.0)
+        nc.scalar.activation(warm_out[:], warm_in[:], TANH)
+
+        for c in range(S // BANK):
+            pre = psum.tile([P, BANK], F32, name=f"pre{c}")
+            nc.tensor.matmul(pre[:], w_sb[:], x_sb[c][:], start=True, stop=True)
+            nc.scalar.activation(h[:, c * BANK : (c + 1) * BANK], pre[:], TANH, bias=b_sb[:])
+
+        nodes = BANK // D
+        for u in range(N // BANK):
+            picked = h[:].indirect(offsets[:, u * BANK // 16 : (u + 1) * BANK // 16])
+            msg = psum.tile([P, BANK], F32, name=f"msg{u}")
+            nc.tensor.matmul(msg[:], w2_sb[:], picked, start=True, stop=True)
+            best = held.tile([P, nodes], F32, name=f"best{u}")
+            nc.vector.tensor_reduce(best[:], msg[:].rearrange("p (v t) -> p v t", t=D),
+                                    mybir.AxisListType.X, mybir.AluOpType.max)
+            nc.sync.dma_start(out[:, u * nodes : (u + 1) * nodes], best[:])

@@ -8,26 +8,30 @@ S = 2048
 N = 1536
 D = 4
 BANK = 512
+PIECE = 256
+CUTS = [0, BANK // 2, BANK, 2 * BANK, 3 * BANK, S]
 FLOPS = 2 * P * P * (S + N)
 
 
 def tile_rows_gcn2_tanh_max_kernel(tc, x, w, b, w2, offs, out):
     nc = tc.nc
+    chunks = list(zip(CUTS[:-1], CUTS[1:]))
     with (
         tc.tile_pool(name="held", bufs=1) as held,
-        tc.psum_pool(name="psum", bufs=1) as psum,
+        tc.psum_pool(name="pre_banks", bufs=4) as pre_banks,
+        tc.psum_pool(name="msg_banks", bufs=4) as msg_banks,
     ):
         w_sb = held.tile([P, P], BF16)
         b_sb = held.tile([P, 1], F32)
         w2_sb = held.tile([P, P], BF16)
         offsets = held.tile([P, N // 16], U16)
-        x_sb = [held.tile([P, BANK], BF16, name=f"x{c}") for c in range(S // BANK)]
+        x_sb = [held.tile([P, hi - lo], BF16, name=f"x{lo}") for lo, hi in chunks]
         h = held.tile([P, S], BF16)
 
-        nc.sync.dma_start(w_sb[:], w)
+        nc.scalar.dma_start(w_sb[:], w)
         nc.scalar.dma_start(b_sb[:], b)
-        for c in range(S // BANK):
-            nc.sync.dma_start(x_sb[c][:], x[:, c * BANK : (c + 1) * BANK])
+        for (lo, hi), x_chunk in zip(chunks, x_sb):
+            nc.sync.dma_start(x_chunk[:], x[:, lo:hi])
         nc.sync.dma_start(w2_sb[:], w2)
         nc.sync.dma_start(offsets[:], offs)
 
@@ -36,15 +40,15 @@ def tile_rows_gcn2_tanh_max_kernel(tc, x, w, b, w2, offs, out):
         nc.vector.memset(warm_in[:], 0.0)
         nc.scalar.activation(warm_out[:], warm_in[:], TANH)
 
-        for c in range(S // BANK):
-            pre = psum.tile([P, BANK], F32, name=f"pre{c}")
-            nc.tensor.matmul(pre[:], w_sb[:], x_sb[c][:], start=True, stop=True)
-            nc.scalar.activation(h[:, c * BANK : (c + 1) * BANK], pre[:], TANH, bias=b_sb[:])
+        for (lo, hi), x_chunk in zip(chunks, x_sb):
+            pre = pre_banks.tile([P, BANK], F32)
+            nc.tensor.matmul(pre[:, : hi - lo], w_sb[:], x_chunk[:], start=True, stop=True)
+            nc.scalar.activation(h[:, lo:hi], pre[:, : hi - lo], TANH, bias=b_sb[:])
 
-        nodes = BANK // D
-        for u in range(N // BANK):
-            picked = h[:].indirect(offsets[:, u * BANK // 16 : (u + 1) * BANK // 16])
-            msg = psum.tile([P, BANK], F32, name=f"msg{u}")
+        nodes = PIECE // D
+        for u in range(N // PIECE):
+            picked = h[:].indirect(offsets[:, u * PIECE // 16 : (u + 1) * PIECE // 16])
+            msg = msg_banks.tile([P, PIECE], F32)
             nc.tensor.matmul(msg[:], w2_sb[:], picked, start=True, stop=True)
             best = held.tile([P, nodes], F32, name=f"best{u}")
             nc.vector.tensor_reduce(best[:], msg[:].rearrange("p (v t) -> p v t", t=D),

@@ -9,13 +9,14 @@ N = 1536
 D = 4
 BANK = 512
 PIECE = 256
-CUTS = [0, BANK // 2, BANK, 2 * BANK, 3 * BANK, S]
+LOAD_CUTS = [0, BANK // 2, BANK, 2 * BANK, 3 * BANK, S]
+LAYER1_CUTS = LOAD_CUTS
+WARM_MATMULS = 10
 FLOPS = 2 * P * P * (S + N)
 
 
 def tile_rows_gcn2_tanh_max_kernel(tc, x, w, b, w2, offs, out):
     nc = tc.nc
-    chunks = list(zip(CUTS[:-1], CUTS[1:]))
     with (
         tc.tile_pool(name="held", bufs=1) as held,
         tc.psum_pool(name="pre_banks", bufs=4) as pre_banks,
@@ -25,32 +26,35 @@ def tile_rows_gcn2_tanh_max_kernel(tc, x, w, b, w2, offs, out):
         b_sb = held.tile([P, 1], F32)
         w2_sb = held.tile([P, P], BF16)
         offsets = held.tile([P, N // 16], U16)
-        x_sb = [held.tile([P, hi - lo], BF16, name=f"x{lo}") for lo, hi in chunks]
+        x_sb = held.tile([P, S], BF16)
         h = held.tile([P, S], BF16)
 
         nc.scalar.dma_start(w_sb[:], w)
         nc.scalar.dma_start(b_sb[:], b)
-        for (lo, hi), x_chunk in zip(chunks, x_sb):
-            nc.sync.dma_start(x_chunk[:], x[:, lo:hi])
+        for lo, hi in zip(LOAD_CUTS[:-1], LOAD_CUTS[1:]):
+            nc.sync.dma_start(x_sb[:, lo:hi], x[:, lo:hi])
         nc.sync.dma_start(w2_sb[:], w2)
         nc.sync.dma_start(offsets[:], offs)
 
-        warm_in = held.tile([P, 1], F32)
+        zeros = held.tile([P, P], BF16)
         warm_out = held.tile([P, 1], F32)
-        nc.vector.memset(warm_in[:], 0.0)
-        nc.scalar.activation(warm_out[:], warm_in[:], TANH)
+        idle_bank = msg_banks.tile([P, P], F32, name="msg")
+        nc.vector.memset(zeros[:], 0.0)
+        nc.scalar.activation(warm_out[:], zeros[:, :1], TANH)
+        for turn in range(WARM_MATMULS):
+            nc.tensor.matmul(idle_bank[:], zeros[:], zeros[:], start=True, stop=True)
 
-        for (lo, hi), x_chunk in zip(chunks, x_sb):
+        for lo, hi in zip(LAYER1_CUTS[:-1], LAYER1_CUTS[1:]):
             pre = pre_banks.tile([P, BANK], F32)
-            nc.tensor.matmul(pre[:, : hi - lo], w_sb[:], x_chunk[:], start=True, stop=True)
+            nc.tensor.matmul(pre[:, : hi - lo], w_sb[:], x_sb[:, lo:hi], start=True, stop=True)
             nc.scalar.activation(h[:, lo:hi], pre[:, : hi - lo], TANH, bias=b_sb[:])
 
         nodes = PIECE // D
+        best = held.tile([P, N // D], F32)
         for u in range(N // PIECE):
             picked = h[:].indirect(offsets[:, u * PIECE // 16 : (u + 1) * PIECE // 16])
             msg = msg_banks.tile([P, PIECE], F32)
             nc.tensor.matmul(msg[:], w2_sb[:], picked, start=True, stop=True)
-            best = held.tile([P, nodes], F32, name=f"best{u}")
-            nc.vector.tensor_reduce(best[:], msg[:].rearrange("p (v t) -> p v t", t=D),
+            nc.vector.tensor_reduce(best[:, u * nodes : (u + 1) * nodes], msg[:].rearrange("p (v t) -> p v t", t=D),
                                     mybir.AxisListType.X, mybir.AluOpType.max)
-            nc.sync.dma_start(out[:, u * nodes : (u + 1) * nodes], best[:])
+            nc.sync.dma_start(out[:, u * nodes : (u + 1) * nodes], best[:, u * nodes : (u + 1) * nodes])

import concourse.mybir as mybir

BF16, F32, U16 = mybir.dt.bfloat16, mybir.dt.float32, mybir.dt.uint16
TANH = mybir.ActivationFunctionType.Tanh

P = 128
S = 2048
N = 1536
D = 4
BANK = 512
PIECE = 256
LOAD_CUTS = [0, BANK // 2, BANK, 2 * BANK, 3 * BANK, S]
LAYER1_CUTS = LOAD_CUTS
WARM_MATMULS = 10
FLOPS = 2 * P * P * (S + N)


def tile_rows_gcn2_tanh_max_kernel(tc, x, w, b, w2, offs, out):
    nc = tc.nc
    with (
        tc.tile_pool(name="held", bufs=1) as held,
        tc.psum_pool(name="pre_banks", bufs=4) as pre_banks,
        tc.psum_pool(name="msg_banks", bufs=4) as msg_banks,
    ):
        w_sb = held.tile([P, P], BF16)
        b_sb = held.tile([P, 1], F32)
        w2_sb = held.tile([P, P], BF16)
        offsets = held.tile([P, N // 16], U16)
        x_sb = held.tile([P, S], BF16)
        h = held.tile([P, S], BF16)

        nc.scalar.dma_start(w_sb[:], w)
        nc.scalar.dma_start(b_sb[:], b)
        for lo, hi in zip(LOAD_CUTS[:-1], LOAD_CUTS[1:]):
            nc.sync.dma_start(x_sb[:, lo:hi], x[:, lo:hi])
        nc.sync.dma_start(w2_sb[:], w2)
        nc.sync.dma_start(offsets[:], offs)

        zeros = held.tile([P, P], BF16)
        warm_out = held.tile([P, 1], F32)
        idle_bank = msg_banks.tile([P, P], F32, name="msg")
        nc.vector.memset(zeros[:], 0.0)
        nc.scalar.activation(warm_out[:], zeros[:, :1], TANH)
        for turn in range(WARM_MATMULS):
            nc.tensor.matmul(idle_bank[:], zeros[:], zeros[:], start=True, stop=True)

        for lo, hi in zip(LAYER1_CUTS[:-1], LAYER1_CUTS[1:]):
            pre = pre_banks.tile([P, BANK], F32)
            nc.tensor.matmul(pre[:, : hi - lo], w_sb[:], x_sb[:, lo:hi], start=True, stop=True)
            nc.scalar.activation(h[:, lo:hi], pre[:, : hi - lo], TANH, bias=b_sb[:])

        nodes = PIECE // D
        best = held.tile([P, N // D], F32)
        for u in range(N // PIECE):
            picked = h[:].indirect(offsets[:, u * PIECE // 16 : (u + 1) * PIECE // 16])
            msg = msg_banks.tile([P, PIECE], F32)
            nc.tensor.matmul(msg[:], w2_sb[:], picked, start=True, stop=True)
            nc.vector.tensor_reduce(best[:, u * nodes : (u + 1) * nodes], msg[:].rearrange("p (v t) -> p v t", t=D),
                                    mybir.AxisListType.X, mybir.AluOpType.max)
            nc.sync.dma_start(out[:, u * nodes : (u + 1) * nodes], best[:, u * nodes : (u + 1) * nodes])
